import numpy as np
import ml_dtypes


def mxq(x, axis, fmt="e4m3"):
    dtype, down = {"e4m3": (ml_dtypes.float8_e4m3fn, 7), "e5m2": (ml_dtypes.float8_e5m2, 14)}[fmt]
    v = np.moveaxis(np.asarray(x, np.float32).astype(ml_dtypes.bfloat16).astype(np.float64), axis, -1)
    blocks = v.reshape(v.shape[:-1] + (-1, 32))
    amax = np.abs(blocks).max(-1, keepdims=True)
    byte = np.maximum(np.where(amax > 0, np.frexp(amax)[1] - 1 + 127, 0) - down, 1)
    scale = np.exp2(byte - 127.0)
    codes = (blocks / scale).astype(np.float32).astype(dtype).astype(np.float64)
    return np.moveaxis((codes * scale).reshape(v.shape), -1, axis)


WIDE = False


def mx_kscale(k):
    if not WIDE:
        return np.ones(k)
    levels = np.array([10, -10, 5, -5, 0])
    if k % 512:
        return np.exp2(np.random.permutation(np.resize(levels, k // 32))).repeat(32)
    a = np.empty((k // 512, 16))
    for p in range(k // 512):
        a[p, :8] = np.random.permutation(np.resize(levels, 8))
        for g in range(8):
            far = levels[np.abs(levels - a[p, g]) >= 10]
            a[p, g + 8] = far[np.random.randint(len(far))]
    return np.exp2(a.ravel()).repeat(32)


def f64(x):
    return np.asarray(x).astype(np.float64)


def striped(idx):
    return np.tile(idx.reshape(-1, 16).T, (8, 1)).astype(np.uint16)


def unstriped(offs):
    return offs[:16].T.reshape(-1).astype(np.int64)


E2M1 = np.array([0.0, 0.5, 1.0, 1.5, 2.0, 3.0, 4.0, 6.0, -0.0, -0.5, -1.0, -1.5, -2.0, -3.0, -4.0, -6.0])


def pack_weight(w, fmt):
    k, n = w.shape
    w = f64(np.asarray(w, np.float32).astype(ml_dtypes.bfloat16)).reshape(k // 32, 32, n)
    amax = np.abs(w).max(1)
    if fmt == "e4m3":
        byte = np.frexp(amax)[1] - 1 + 127 - 7
    else:
        mant, ex = np.frexp(amax / 6.0)
        byte = np.where(mant > 0.5, ex, ex - 1) + 127
    byte = np.clip(np.where(amax > 0, byte, 1), 1, 254)
    scaled = (w * np.exp2(127.0 - byte)[:, None, :]).reshape(k, n).astype(np.float32)
    by_word = np.ascontiguousarray(scaled.reshape(k // 512, 128, 4, n).transpose(0, 1, 3, 2))
    if fmt == "e4m3":
        words = by_word.astype(ml_dtypes.float8_e4m3fn).view(np.uint8)
    else:
        c = by_word.astype(ml_dtypes.float4_e2m1fn).view(np.uint8) & 0xF
        words = (c[..., 0::2] | (c[..., 1::2] << 4)).reshape(k // 512, 128, 2 * n)
    return np.ascontiguousarray(words), np.ascontiguousarray(byte.astype(np.uint8).reshape(k // 512, 16, n))


def unpack_weight(words, scales, fmt):
    g, _, n = scales.shape
    words = np.ascontiguousarray(words).reshape(g, 128, n, -1)
    if fmt == "e4m3":
        vals = words.view(ml_dtypes.float8_e4m3fn).astype(np.float64)
    else:
        nib = np.empty((g, 128, n, 4), np.uint8)
        nib[..., 0::2] = words & 0xF
        nib[..., 1::2] = words >> 4
        vals = E2M1[nib]
    vals = vals * np.repeat(np.exp2(scales.astype(np.float64) - 127.0), 8, axis=1)[..., None]
    return vals.transpose(0, 1, 3, 2).reshape(g * 512, n)


def relu(v):
    return np.maximum(v, 0.0)


K, T, E, C, H, N = 512, 768, 8, 128, 512, 384
TOP = 4
PAD = 64


def by_expert(wq, xq):
    return np.concatenate([wq[e].T @ xq[:, e * C:(e + 1) * C] for e in range(E)], axis=1)


def setup_inputs():
    n = np.random.standard_normal
    s = mx_kscale(K)[:, None]
    u = mx_kscale(H)
    slot_token = np.empty(E * C, np.int64); pos = np.tile(E * C + np.arange(T) % PAD, (TOP, 1)); taken = np.zeros(T, np.int64)
    liked = np.random.randn(T)
    for e in np.random.permutation(E):
        free = np.flatnonzero(taken < TOP); pick = np.random.permutation(free[np.argsort(-(liked[free] + np.random.gumbel(size=free.size)))[:C]]); slot_token[e * C:(e + 1) * C] = pick
        pos[taken[pick], pick] = e * C + np.arange(C); taken[pick] += 1
    g = np.random.uniform(0.2, 0.8, (TOP, T))
    x = pack_weight(n((K, T)) * s, "e4m3")
    return {
        "x_words": x[0],
        "x_scales": x[1],
        "w1": (n((E, K, H)) / np.sqrt(K) / s[None]).astype(np.float32),
        "w3": (n((E, K, H)) / np.sqrt(K) / s[None] * u[None, None, :]).astype(np.float32),
        "w2": (n((E, H, N)) / np.sqrt(H) / u[None, :, None]).astype(np.float32),
        "gate": np.stack([np.tile(r, (N, 1)) for r in g]).astype(np.float32),
        "offs": striped(slot_token),
        "pos1": striped(pos[0]),
        "pos2": striped(pos[1]),
        "pos3": striped(pos[2]),
        "pos4": striped(pos[3]),
    }


def reference(x_words, x_scales, w1, w3, w2, gate, offs, pos1, pos2, pos3, pos4):
    idx = unstriped(offs)
    xq = unpack_weight(x_words, x_scales, "e4m3")[:, idx]
    h = relu(by_expert(mxq(f64(w1), 1, "e4m3"), xq))
    h = h * by_expert(mxq(f64(w3), 1, "e4m3"), xq)
    y = by_expert(mxq(f64(w2), 1, "e4m3"), mxq(h, 0, "e4m3"))
    y = np.concatenate([y, np.zeros((N, PAD))], axis=1)
    return sum(f64(gate[r]) * y[:, unstriped(p)] for r, p in enumerate((pos1, pos2, pos3, pos4)))

@@ -1,0 +1,323 @@
+from contextlib import ExitStack
+
+import concourse.mybir as mybir
+from concourse.masks import make_identity
+
+K, T, E, C, H, N = 512, 768, 8, 128, 512, 384
+TOP = 4
+PAD = 64
+SLOTS = E * C
+FLOPS = 2 * SLOTS * (2 * K * H + H * N)
+
+F32 = mybir.dt.float32
+BF16 = mybir.dt.bfloat16
+I32 = mybir.dt.int32
+U32 = mybir.dt.uint32
+U16 = mybir.dt.uint16
+U8 = mybir.dt.uint8
+FP8X4 = mybir.dt.float8_e4m3fn_x4
+ACT = mybir.ActivationFunctionType
+ALU = mybir.AluOpType
+
+P = 128
+PACK = 4
+BLOCKS = N // P
+TOKEN_BLOCKS = T // P
+GATHER = 512
+CHUNK = 256
+RAW_BUFS = 14
+GROUP = 4
+VECTOR_CASTS = ((0, 7), (1, 4), (2, 4))
+
+
+def tile_moe_ecr_glu_relu_kernel(
+    tc, x_words, x_scales, w1, w3, w2, gate, offs, pos1, pos2, pos3, pos4, out
+):
+    nc = tc.nc
+    with ExitStack() as ctx:
+        lists = ctx.enter_context(tc.tile_pool(name="lists", bufs=1))
+        keep = ctx.enter_context(tc.tile_pool(name="keep", bufs=1))
+        raw_pool = ctx.enter_context(tc.tile_pool(name="raw", bufs=RAW_BUFS))
+        stage = ctx.enter_context(tc.tile_pool(name="stage", bufs=3))
+        picks = ctx.enter_context(tc.tile_pool(name="picks", bufs=8))
+        wide_psum = ctx.enter_context(tc.psum_pool(name="wide_psum", bufs=4))
+        sum_psum = ctx.enter_context(tc.psum_pool(name="sum_psum", bufs=2))
+
+        def column_parts(e):
+            parts = 2 if e == E - 1 else 1
+            return [slice(i * H // parts, (i + 1) * H // parts) for i in range(parts)]
+
+        def load_first(w, e):
+            raw = raw_pool.tile([P, PACK, H], F32, name="raw", align_bytes=64)
+            rows = w[e].rearrange("(p j) c -> p j c", j=PACK)
+            for cols in column_parts(e):
+                nc.sync.dma_start(out=raw[:, :, cols], in_=rows[:, :, cols])
+            return raw
+
+        w2_rows = w2.rearrange("e (p j) n -> p j e n", j=PACK)
+
+        def load_second(block, e0):
+            raw = raw_pool.tile([P, GROUP, PACK, P], F32, name="raw", align_bytes=64)
+            for e in range(e0, e0 + GROUP):
+                nc.sync.dma_start(out=raw[:, e - e0, :, :], in_=w2_rows[:, :, e, block * P : (block + 1) * P])
+            return raw
+
+        def copy_on(engine, dst, src):
+            if engine is nc.vector:
+                nc.vector.tensor_copy(out=dst, in_=src)
+            else:
+                nc.scalar.copy(out=dst, in_=src)
+
+        def quantize(values, width, pool, name):
+            codes = pool.tile([P, width], U32, name=name + "_codes", align_bytes=64)
+            scales = pool.tile([P, width], U8, name=name + "_scales", align_bytes=64)
+            nc.vector.quantize_mx(out=codes[:].bitcast(FP8X4), scales=scales[:], in_=values)
+            return codes, scales
+
+        def mx(dst, stationary, s_cols, moving, m_cols):
+            nc.tensor.matmul_mx(
+                out=dst,
+                lhsT=stationary[0][:, s_cols].bitcast(FP8X4),
+                lhsT_scale=stationary[1][:, s_cols],
+                rhs=moving[0][:, m_cols].bitcast(FP8X4),
+                rhs_scale=moving[1][:, m_cols],
+                start=True,
+                stop=True,
+            )
+
+        token_scales = keep.tile([P, T], U8, name="token_scales", align_bytes=64)
+        nc.gpsimd.memset(token_scales[:].bitcast(I32), 0)
+        slot_list = lists.tile([P, SLOTS // 16], U16, name="slot_list")
+        nc.sync.dma_start(slot_list[:], offs)
+        token_words = keep.tile([P, T], I32, name="token_words", align_bytes=64)
+        nc.sync.dma_start(out=token_words[:], in_=x_words[0].rearrange("p t r -> p (t r)").bitcast(I32))
+        for q in range(4):
+            nc.sync.dma_start(
+                out=token_scales[32 * q : 32 * q + 4, :].bitcast(I32),
+                in_=x_scales[0, 4 * q : 4 * q + 4, :].bitcast(I32),
+            )
+        first_raw = {}
+        for e in range(2):
+            first_raw[0, e] = load_first(w1, e)
+            first_raw[1, e] = load_first(w3, e)
+
+        identity = keep.tile([P, P], F32, name="identity")
+        make_identity(nc, identity[:])
+        gate_rows = keep.tile([P, P], F32, name="gate_rows")
+        nc.gpsimd.memset(gate_rows[:], 0.0)
+        results = []
+        for block in range(BLOCKS):
+            result = keep.tile([P, SLOTS + PAD], F32, name="result%d" % block)
+            nc.gpsimd.memset(result[:, SLOTS:], 0.0)
+            results.append(result)
+
+        slot_tokens = []
+        for g in range(SLOTS // GATHER):
+            piece = slot_list[:, g * GATHER // 16 : (g + 1) * GATHER // 16]
+            words = keep.tile([P, GATHER], U32, name="slot_words%d" % g, align_bytes=64)
+            scales = keep.tile([P, GATHER], U8, name="slot_scales%d" % g, align_bytes=64)
+            nc.vector.tensor_copy(out=words[:], in_=token_words[:].bitcast(U32).indirect(piece))
+            nc.vector.tensor_copy(out=scales[:], in_=token_scales[:].indirect(piece))
+            slot_tokens.append((words, scales))
+
+        back_lists = []
+        for r, pos in enumerate((pos1, pos2, pos3, pos4)):
+            back_list = lists.tile([P, T // 16], U16, name="back_list%d" % r)
+            nc.sync.dma_start(back_list[:], pos)
+            back_lists.append(back_list)
+        gate_step = BLOCKS * P + 1
+        gate_count = TOP * TOKEN_BLOCKS
+        nc.sync.dma_start(
+            out=gate_rows[0:gate_count, :],
+            in_=gate.rearrange("r n (b p) -> (r n b) p", p=P)[0 : (gate_count - 1) * gate_step + 1 : gate_step, :],
+        )
+        gate_turned = sum_psum.tile([P, P], F32, name="back")
+        nc.tensor.transpose(gate_turned[:], gate_rows[:], identity[:])
+        gates = keep.tile([P, gate_count], F32, name="gates")
+        nc.scalar.copy(out=gates[:], in_=gate_turned[:, 0:gate_count])
+
+        scalar_stage = [keep.tile([P, H * PACK], BF16, name="scalar_stage%d" % i, align_bytes=64) for i in range(2)]
+        vector_stage = keep.tile([P, H * PACK], BF16, name="vector_stage", align_bytes=64)
+        scalar_turns = []
+
+        def next_stage(engine):
+            if engine is nc.vector:
+                return vector_stage
+            scalar_turns.append(0)
+            return scalar_stage[len(scalar_turns) % len(scalar_stage)]
+
+        def round_first(raw, engine, e):
+            rounded = next_stage(engine)
+            for cols in column_parts(e):
+                copy_on(
+                    engine,
+                    rounded[:].rearrange("p (t m j) -> p m j t", t=PACK, j=PACK)[
+                        :, cols.start // PACK : cols.stop // PACK, :, :
+                    ],
+                    raw[:, :, cols].rearrange("p j (m t) -> p m j t", t=PACK),
+                )
+            return rounded
+
+        def first_product(rounded, e):
+            weight = quantize(rounded[:], H, stage, "first")
+            sums = wide_psum.tile([P, PACK, C], F32, name="wide")
+            tokens = slot_tokens[e * C // GATHER]
+            cols = slice(e * C % GATHER, e * C % GATHER + C)
+            for t in range(PACK):
+                mx(sums[:, t, :], weight, slice(t * P, (t + 1) * P), tokens, cols)
+            return sums
+
+        hidden = []
+        second_raw = {}
+
+        def rectify(a, relu_a):
+            nc.scalar.activation(
+                out=relu_a.rearrange("p (s t) -> p s t", t=PACK), in_=a[:].rearrange("p t s -> p s t"), func=ACT.Relu
+            )
+
+        def gated_product(relu_a, b, h):
+            nc.vector.tensor_tensor(
+                out=h.rearrange("p (s t) -> p s t", t=PACK),
+                in0=b[:].rearrange("p t s -> p s t"),
+                in1=relu_a.rearrange("p (s t) -> p s t", t=PACK),
+                op=ALU.mult,
+            )
+
+        def first_layer(e, pending):
+            rounded_w1 = round_first(first_raw[0, e], nc.scalar, e)
+            if pending:
+                relu_a = first_raw[0, e][:, 0, :]
+                rectify(pending[0], relu_a)
+            a = first_product(rounded_w1, e)
+            rounded_w3 = round_first(first_raw[1, e], nc.vector, e)
+            if pending and e < E - 1:
+                h = first_raw[1, e][:, 0, 0 : C * PACK // 2].bitcast(BF16)
+                gated_product(relu_a, pending[1], h)
+            b = first_product(rounded_w3, e)
+            if pending and e == E - 1:
+                h = first_raw[1, e][:, 0, 0 : C * PACK // 2].bitcast(BF16)
+                gated_product(relu_a, pending[1], h)
+            if pending:
+                hidden.append(quantize(h, C, keep, "hidden%d" % (e - 1)))
+            return a, b
+
+        def finish_first_layer(pending, relu_a):
+            rectify(pending[0], relu_a)
+            h = first_raw[1, E - 1][:, 1, 0 : C * PACK // 2].bitcast(BF16)
+            gated_product(relu_a, pending[1], h)
+            hidden.append(quantize(h, C, keep, "hidden%d" % (E - 1)))
+
+        def second_layer(block, e0, count, experts_a_step, copy_engine):
+            raw = second_raw[block, e0 - e0 % GROUP]
+            sums = sum_psum.tile([P, count, C], F32, name="y")
+            for s in range(0, count, experts_a_step):
+                engine = nc.vector if (block, e0 + s) in VECTOR_CASTS else nc.scalar
+                rounded = next_stage(engine)[:, 0 : experts_a_step * P * PACK]
+                at = (e0 + s) % GROUP
+                copy_on(
+                    engine,
+                    rounded.rearrange("p (e c i j) -> p e c j i", e=experts_a_step, i=4, j=PACK),
+                    raw[:, at : at + experts_a_step, :, :].rearrange("p e j (c i) -> p e c j i", i=4),
+                )
+                weight = quantize(rounded, experts_a_step * P, stage, "second")
+                for d in range(experts_a_step):
+                    mx(sums[:, s + d, :], weight, slice(d * P, (d + 1) * P), hidden[e0 + s + d], slice(0, C))
+            copy_on(
+                copy_engine, results[block][:, e0 * C : (e0 + count) * C], sums[:].rearrange("p e s -> p (e s)")
+            )
+            return rounded
+
+        def combine(block, t0, spent):
+            blocks_in_chunk = CHUNK // P
+            weighted = stage.tile([P, blocks_in_chunk, TOP, P], F32, name="weighted")
+            for pair in range(0, TOP, 2):
+                turned = wide_psum.tile([P, 2, blocks_in_chunk, P], F32, name="wide")
+                for r in (pair, pair + 1):
+                    if r == 0 and spent is not None:
+                        picked = spent.bitcast(F32)[:, 0:CHUNK]
+                    else:
+                        picked = picks.tile([P, CHUNK], F32, name="picked")[:]
+                    offsets = back_lists[r][:, t0 // 16 : (t0 + CHUNK) // 16]
+                    nc.vector.tensor_copy(out=picked, in_=results[block][:].indirect(offsets))
+                    for b in range(blocks_in_chunk):
+                        nc.tensor.transpose(turned[:, r - pair, b, :], picked[:, b * P : (b + 1) * P], identity[:])
+                for r in (pair, pair + 1):
+                    for b in range(blocks_in_chunk):
+                        col = r * TOKEN_BLOCKS + t0 // P + b
+                        nc.scalar.activation(
+                            out=weighted[:, b, r, :],
+                            in_=turned[:, r - pair, b, :],
+                            func=ACT.Copy,
+                            scale=gates[:, col : col + 1],
+                        )
+            total = sum_psum.tile([P, blocks_in_chunk, P], F32, name="back")
+            for b in range(blocks_in_chunk):
+                for r in range(TOP):
+                    nc.tensor.matmul(
+                        total[:, b, :],
+                        lhsT=weighted[:, b, r, :],
+                        rhs=identity[:],
+                        start=(r == 0),
+                        stop=(r == TOP - 1),
+                        is_transpose=True,
+                    )
+            done = stage.tile([P, CHUNK], F32, name="done")
+            nc.scalar.copy(out=done[:], in_=total[:].rearrange("p b t -> p (b t)"))
+            nc.sync.dma_start(out=out[block * P : (block + 1) * P, t0 : t0 + CHUNK], in_=done[:])
+
+        def combine_last(block, t0):
+            blocks_in_chunk = CHUNK // P
+            totals = [sum_psum.tile([P, P], F32, name="back") for b in range(blocks_in_chunk)]
+            for r in range(TOP):
+                picked = picks.tile([P, CHUNK], F32, name="picked")
+                offsets = back_lists[r][:, t0 // 16 : (t0 + CHUNK) // 16]
+                nc.vector.tensor_copy(out=picked[:], in_=results[block][:].indirect(offsets))
+                for b in range(blocks_in_chunk):
+                    turned = wide_psum.tile([P, P], F32, name="wide")
+                    nc.tensor.transpose(turned[:], picked[:, b * P : (b + 1) * P], identity[:])
+                    weighted = picks.tile([P, P], F32, name="weighted_last")
+                    col = r * TOKEN_BLOCKS + t0 // P + b
+                    if r == TOP - 1 and b == 0:
+                        nc.vector.tensor_scalar(
+                            out=weighted[:], in0=turned[:], scalar1=gates[:, col : col + 1], scalar2=None, op0=ALU.mult
+                        )
+                    else:
+                        nc.scalar.activation(
+                            out=weighted[:], in_=turned[:], func=ACT.Copy, scale=gates[:, col : col + 1]
+                        )
+                    nc.tensor.matmul(
+                        totals[b][:],
+                        lhsT=weighted[:],
+                        rhs=identity[:],
+                        start=(r == 0),
+                        stop=(r == TOP - 1),
+                        is_transpose=True,
+                    )
+            done = stage.tile([P, CHUNK], F32, name="done")
+            for b in range(blocks_in_chunk):
+                copy_on(nc.vector if b == 0 else nc.scalar, done[:, b * P : (b + 1) * P], totals[b][:])
+            nc.sync.dma_start(out=out[block * P : (block + 1) * P, t0 : t0 + CHUNK], in_=done[:])
+
+        pending = None
+        for e in range(E):
+            if e + 2 < E:
+                first_raw[0, e + 2] = load_first(w1, e + 2)
+                first_raw[1, e + 2] = load_first(w3, e + 2)
+            if e == E - 2:
+                for block in range(BLOCKS):
+                    for e0 in range(0, E, GROUP):
+                        second_raw[block, e0] = load_second(block, e0)
+            pending = first_layer(e, pending)
+        second_layer(0, 0, GROUP, 2, nc.scalar)
+        finish_first_layer(pending, second_raw[0, 0][:, 1, :, :].rearrange("p j n -> p (j n)"))
+        second_layer(0, GROUP, GROUP - 1, 1, nc.scalar)
+        second_layer(0, E - 1, 1, 1, nc.vector)
+        for block in range(BLOCKS):
+            spent = None
+            for step, t0 in enumerate(range(0, T, CHUNK)):
+                if block + 1 == BLOCKS and t0 + CHUNK == T:
+                    combine_last(block, t0)
+                else:
+                    combine(block, t0, spent)
+                if block + 1 < BLOCKS and step < E // GROUP:
+                    spent = second_layer(block + 1, step * GROUP, GROUP, 2, nc.scalar)

@@ -25,9 +25,9 @@ BLOCKS = N // P
 TOKEN_BLOCKS = T // P
 GATHER = 512
 CHUNK = 256
-RAW_BUFS = 14
+RAW_BUFS = 12
 GROUP = 4
-VECTOR_CASTS = ((0, 7), (1, 4), (2, 4))
+VECTOR_CASTS = ((0, 7),)
 
 
 def tile_moe_ecr_glu_relu_kernel(
@@ -40,8 +40,11 @@ def tile_moe_ecr_glu_relu_kernel(
         raw_pool = ctx.enter_context(tc.tile_pool(name="raw", bufs=RAW_BUFS))
         stage = ctx.enter_context(tc.tile_pool(name="stage", bufs=3))
         picks = ctx.enter_context(tc.tile_pool(name="picks", bufs=8))
+        weights = ctx.enter_context(tc.tile_pool(name="weights", bufs=2))
         wide_psum = ctx.enter_context(tc.psum_pool(name="wide_psum", bufs=4))
         sum_psum = ctx.enter_context(tc.psum_pool(name="sum_psum", bufs=2))
+        slot_psum = ctx.enter_context(tc.psum_pool(name="slot_psum", bufs=1))
+        slot_banks = [slot_psum.tile([P, GROUP, C], F32, name="slot_bank%d" % i) for i in range(2)]
 
         def column_parts(e):
             parts = 2 if e == E - 1 else 1
@@ -87,6 +90,14 @@ def tile_moe_ecr_glu_relu_kernel(
 
         token_scales = keep.tile([P, T], U8, name="token_scales", align_bytes=64)
         nc.gpsimd.memset(token_scales[:].bitcast(I32), 0)
+        gate_rows = keep.tile([P, P], F32, name="gate_rows")
+        nc.gpsimd.memset(gate_rows[:], 0.0)
+        gate_step = BLOCKS * P + 1
+        gate_count = TOP * TOKEN_BLOCKS
+        nc.scalar.dma_start(
+            out=gate_rows[0:gate_count, :],
+            in_=gate.rearrange("r n (b p) -> (r n b) p", p=P)[0 : (gate_count - 1) * gate_step + 1 : gate_step, :],
+        )
         slot_list = lists.tile([P, SLOTS // 16], U16, name="slot_list")
         nc.sync.dma_start(slot_list[:], offs)
         token_words = keep.tile([P, T], I32, name="token_words", align_bytes=64)
@@ -103,8 +114,19 @@ def tile_moe_ecr_glu_relu_kernel(
 
         identity = keep.tile([P, P], F32, name="identity")
         make_identity(nc, identity[:])
-        gate_rows = keep.tile([P, P], F32, name="gate_rows")
-        nc.gpsimd.memset(gate_rows[:], 0.0)
+        gate_turned = sum_psum.tile([P, P], F32, name="back")
+        nc.tensor.transpose(gate_turned[:], gate_rows[:], identity[:])
+        gate_columns = keep.tile([P, gate_count], F32, name="gate_columns")
+        nc.scalar.copy(out=gate_columns[:], in_=gate_turned[:, 0:gate_count])
+        gates = keep.tile([P, TOP * T], F32, name="gates")
+        for q0 in range(0, gate_count, 4):
+            spread = sum_psum.tile([P, 4, P], F32, name="back")
+            for q in range(q0, q0 + 4):
+                nc.tensor.transpose(
+                    spread[:, q - q0, :], gate_columns[:, q : q + 1].to_broadcast([P, P]), identity[:]
+                )
+            nc.scalar.copy(out=gates[:, q0 * P : (q0 + 4) * P], in_=spread[:].rearrange("p q t -> p (q t)"))
+
         results = []
         for block in range(BLOCKS):
             result = keep.tile([P, SLOTS + PAD], F32, name="result%d" % block)
@@ -125,17 +147,6 @@ def tile_moe_ecr_glu_relu_kernel(
             back_list = lists.tile([P, T // 16], U16, name="back_list%d" % r)
             nc.sync.dma_start(back_list[:], pos)
             back_lists.append(back_list)
-        gate_step = BLOCKS * P + 1
-        gate_count = TOP * TOKEN_BLOCKS
-        nc.sync.dma_start(
-            out=gate_rows[0:gate_count, :],
-            in_=gate.rearrange("r n (b p) -> (r n b) p", p=P)[0 : (gate_count - 1) * gate_step + 1 : gate_step, :],
-        )
-        gate_turned = sum_psum.tile([P, P], F32, name="back")
-        nc.tensor.transpose(gate_turned[:], gate_rows[:], identity[:])
-        gates = keep.tile([P, gate_count], F32, name="gates")
-        nc.scalar.copy(out=gates[:], in_=gate_turned[:, 0:gate_count])
-
         scalar_stage = [keep.tile([P, H * PACK], BF16, name="scalar_stage%d" % i, align_bytes=64) for i in range(2)]
         vector_stage = keep.tile([P, H * PACK], BF16, name="vector_stage", align_bytes=64)
         scalar_turns = []
@@ -207,96 +218,102 @@ def tile_moe_ecr_glu_relu_kernel(
             gated_product(relu_a, pending[1], h)
             hidden.append(quantize(h, C, keep, "hidden%d" % (E - 1)))
 
-        def second_layer(block, e0, count, experts_a_step, copy_engine):
+        def spent_raw(block, e0):
+            return second_raw[block, 0] if e0 >= GROUP else second_raw[block - 1, GROUP]
+
+        def second_step(block, e0, count, sums):
             raw = second_raw[block, e0 - e0 % GROUP]
-            sums = sum_psum.tile([P, count, C], F32, name="y")
-            for s in range(0, count, experts_a_step):
-                engine = nc.vector if (block, e0 + s) in VECTOR_CASTS else nc.scalar
-                rounded = next_stage(engine)[:, 0 : experts_a_step * P * PACK]
-                at = (e0 + s) % GROUP
-                copy_on(
-                    engine,
-                    rounded.rearrange("p (e c i j) -> p e c j i", e=experts_a_step, i=4, j=PACK),
-                    raw[:, at : at + experts_a_step, :, :].rearrange("p e j (c i) -> p e c j i", i=4),
-                )
-                weight = quantize(rounded, experts_a_step * P, stage, "second")
-                for d in range(experts_a_step):
-                    mx(sums[:, s + d, :], weight, slice(d * P, (d + 1) * P), hidden[e0 + s + d], slice(0, C))
+            engine = nc.vector if (block, e0) in VECTOR_CASTS else nc.scalar
+            if block > 0:
+                rounded = spent_raw(block, e0)[:, 2:4, :, :].rearrange("p e j n -> p (e j n)").bitcast(BF16)
+            else:
+                rounded = next_stage(engine)[:, 0 : count * P * PACK]
+            at = e0 % GROUP
             copy_on(
-                copy_engine, results[block][:, e0 * C : (e0 + count) * C], sums[:].rearrange("p e s -> p (e s)")
+                engine,
+                rounded.rearrange("p (e c i j) -> p e c j i", e=count, i=4, j=PACK),
+                raw[:, at : at + count, :, :].rearrange("p e j (c i) -> p e c j i", i=4),
             )
+            weight = quantize(rounded, count * P, stage, "second")
+            for d in range(count):
+                mx(sums[:, d, :], weight, slice(d * P, (d + 1) * P), hidden[e0 + d], slice(0, C))
             return rounded
 
-        def combine(block, t0, spent):
-            blocks_in_chunk = CHUNK // P
-            weighted = stage.tile([P, blocks_in_chunk, TOP, P], F32, name="weighted")
-            for pair in range(0, TOP, 2):
-                turned = wide_psum.tile([P, 2, blocks_in_chunk, P], F32, name="wide")
-                for r in (pair, pair + 1):
-                    if r == 0 and spent is not None:
-                        picked = spent.bitcast(F32)[:, 0:CHUNK]
-                    else:
-                        picked = picks.tile([P, CHUNK], F32, name="picked")[:]
-                    offsets = back_lists[r][:, t0 // 16 : (t0 + CHUNK) // 16]
-                    nc.vector.tensor_copy(out=picked, in_=results[block][:].indirect(offsets))
-                    for b in range(blocks_in_chunk):
-                        nc.tensor.transpose(turned[:, r - pair, b, :], picked[:, b * P : (b + 1) * P], identity[:])
-                for r in (pair, pair + 1):
-                    for b in range(blocks_in_chunk):
-                        col = r * TOKEN_BLOCKS + t0 // P + b
-                        nc.scalar.activation(
-                            out=weighted[:, b, r, :],
-                            in_=turned[:, r - pair, b, :],
-                            func=ACT.Copy,
-                            scale=gates[:, col : col + 1],
-                        )
-            total = sum_psum.tile([P, blocks_in_chunk, P], F32, name="back")
+        def second_layer(block, e0, count, experts_a_step, copy_engine, bank):
+            sums = slot_banks[bank][:, 0:count, :]
+            for s in range(0, count, experts_a_step):
+                second_step(block, e0 + s, experts_a_step, sums[:, s : s + experts_a_step, :])
+            copy_on(
+                copy_engine, results[block][:, e0 * C : (e0 + count) * C], sums.rearrange("p e s -> p (e s)")
+            )
+
+
+        def next_block_pair(block, group):
+            e0 = group * GROUP
+            sums = slot_banks[group]
+            spent = second_step(block, e0, GROUP, sums[:])
+            nc.scalar.copy(
+                out=results[block][:, e0 * C : (e0 + GROUP) * C], in_=sums[:].rearrange("p e s -> p (e s)")
+            )
+            return spent
+
+        spent_stage = {}
+
+        def weighted_pick(picked, block, r, t0, width):
+            offsets = back_lists[r][:, t0 // 16 : (t0 + width) // 16]
+            nc.vector.tensor_tensor(
+                out=picked,
+                in0=results[block][:].indirect(offsets),
+                in1=gates[:, r * T + t0 : r * T + t0 + width],
+                op=ALU.mult,
+            )
+
+        def combine(block, t0, width, casts, gather_after):
+            blocks_in_chunk = width // P
+            for pair in casts:
+                next_block_pair(*pair)
+            products = []
+            for r in range(TOP):
+                if r in gather_after:
+                    picked = spent_raw(block + 1, gather_after[r] * GROUP)[:, r, :, :].rearrange("p j n -> p (j n)")[:, 0:width]
+                else:
+                    picked = picks.tile([P, width], F32, name="picked")[:]
+                weighted_pick(picked, block, r, t0, width)
+                products.append(picked)
+            if casts:
+                turned = slot_banks[1][:, 0:blocks_in_chunk, :]
+            else:
+                turned = wide_psum.tile([P, blocks_in_chunk, P], F32, name="wide")[:]
             for b in range(blocks_in_chunk):
                 for r in range(TOP):
                     nc.tensor.matmul(
-                        total[:, b, :],
-                        lhsT=weighted[:, b, r, :],
+                        turned[:, b, :],
+                        lhsT=products[r][:, b * P : (b + 1) * P],
                         rhs=identity[:],
                         start=(r == 0),
                         stop=(r == TOP - 1),
                         is_transpose=True,
                     )
-            done = stage.tile([P, CHUNK], F32, name="done")
+            room = weights.tile([P, blocks_in_chunk, P], F32, name="weighted")
+            nc.scalar.copy(out=room[:], in_=turned)
+            total = sum_psum.tile([P, blocks_in_chunk, P], F32, name="back")
+            for b in range(blocks_in_chunk):
+                nc.tensor.transpose(total[:, b, :], room[:, b, :], identity[:])
+            done = stage.tile([P, width], F32, name="done")
             nc.scalar.copy(out=done[:], in_=total[:].rearrange("p b t -> p (b t)"))
-            nc.sync.dma_start(out=out[block * P : (block + 1) * P, t0 : t0 + CHUNK], in_=done[:])
+            nc.sync.dma_start(out=out[block * P : (block + 1) * P, t0 : t0 + width], in_=done[:])
 
         def combine_last(block, t0):
-            blocks_in_chunk = CHUNK // P
-            totals = [sum_psum.tile([P, P], F32, name="back") for b in range(blocks_in_chunk)]
+            total = None
             for r in range(TOP):
                 picked = picks.tile([P, CHUNK], F32, name="picked")
-                offsets = back_lists[r][:, t0 // 16 : (t0 + CHUNK) // 16]
-                nc.vector.tensor_copy(out=picked[:], in_=results[block][:].indirect(offsets))
-                for b in range(blocks_in_chunk):
-                    turned = wide_psum.tile([P, P], F32, name="wide")
-                    nc.tensor.transpose(turned[:], picked[:, b * P : (b + 1) * P], identity[:])
-                    weighted = picks.tile([P, P], F32, name="weighted_last")
-                    col = r * TOKEN_BLOCKS + t0 // P + b
-                    if r == TOP - 1 and b == 0:
-                        nc.vector.tensor_scalar(
-                            out=weighted[:], in0=turned[:], scalar1=gates[:, col : col + 1], scalar2=None, op0=ALU.mult
-                        )
-                    else:
-                        nc.scalar.activation(
-                            out=weighted[:], in_=turned[:], func=ACT.Copy, scale=gates[:, col : col + 1]
-                        )
-                    nc.tensor.matmul(
-                        totals[b][:],
-                        lhsT=weighted[:],
-                        rhs=identity[:],
-                        start=(r == 0),
-                        stop=(r == TOP - 1),
-                        is_transpose=True,
-                    )
-            done = stage.tile([P, CHUNK], F32, name="done")
-            for b in range(blocks_in_chunk):
-                copy_on(nc.vector if b == 0 else nc.scalar, done[:, b * P : (b + 1) * P], totals[b][:])
-            nc.sync.dma_start(out=out[block * P : (block + 1) * P, t0 : t0 + CHUNK], in_=done[:])
+                weighted_pick(picked[:], block, r, t0, CHUNK)
+                if r > 0:
+                    more = stage.tile([P, CHUNK], F32, name="done")
+                    nc.vector.tensor_tensor(out=more[:], in0=total[:], in1=picked[:], op=ALU.add)
+                    picked = more
+                total = picked
+            nc.sync.dma_start(out=out[block * P : (block + 1) * P, t0 : t0 + CHUNK], in_=total[:])
 
         pending = None
         for e in range(E):
@@ -308,16 +325,14 @@ def tile_moe_ecr_glu_relu_kernel(
                     for e0 in range(0, E, GROUP):
                         second_raw[block, e0] = load_second(block, e0)
             pending = first_layer(e, pending)
-        second_layer(0, 0, GROUP, 2, nc.scalar)
+        second_layer(0, 0, GROUP, 2, nc.scalar, 0)
         finish_first_layer(pending, second_raw[0, 0][:, 1, :, :].rearrange("p j n -> p (j n)"))
-        second_layer(0, GROUP, GROUP - 1, 1, nc.scalar)
-        second_layer(0, E - 1, 1, 1, nc.vector)
-        for block in range(BLOCKS):
-            spent = None
-            for step, t0 in enumerate(range(0, T, CHUNK)):
-                if block + 1 == BLOCKS and t0 + CHUNK == T:
-                    combine_last(block, t0)
-                else:
-                    combine(block, t0, spent)
-                if block + 1 < BLOCKS and step < E // GROUP:
-                    spent = second_layer(block + 1, step * GROUP, GROUP, 2, nc.scalar)
+        second_layer(0, GROUP, 2, 1, nc.scalar, 1)
+        second_layer(0, E - 2, 2, 1, nc.vector, 0)
+        for block in range(BLOCKS - 1):
+            pairs = [(block + 1, pair) for pair in range(E // GROUP)]
+            combine(block, 0, T // 2, pairs, {2: 0, 3: 0})
+            combine(block, T // 2, T // 2, [], {0: 1, 1: 1, 2: 1, 3: 1})
+        for t0 in range(0, T - CHUNK, CHUNK):
+            combine(BLOCKS - 1, t0, CHUNK, [], {})
+        combine_last(BLOCKS - 1, T - CHUNK)

from contextlib import ExitStack

import concourse.mybir as mybir
from concourse.masks import make_identity

K, T, E, C, H, N = 512, 768, 8, 128, 512, 384
TOP = 4
PAD = 64
SLOTS = E * C
FLOPS = 2 * SLOTS * (2 * K * H + H * N)

F32 = mybir.dt.float32
BF16 = mybir.dt.bfloat16
I32 = mybir.dt.int32
U32 = mybir.dt.uint32
U16 = mybir.dt.uint16
U8 = mybir.dt.uint8
FP8X4 = mybir.dt.float8_e4m3fn_x4
ACT = mybir.ActivationFunctionType
ALU = mybir.AluOpType

P = 128
PACK = 4
BLOCKS = N // P
TOKEN_BLOCKS = T // P
GATHER = 512
CHUNK = 256
RAW_BUFS = 12
GROUP = 4
VECTOR_CASTS = ((0, 7),)


def tile_moe_ecr_glu_relu_kernel(
    tc, x_words, x_scales, w1, w3, w2, gate, offs, pos1, pos2, pos3, pos4, out
):
    nc = tc.nc
    with ExitStack() as ctx:
        lists = ctx.enter_context(tc.tile_pool(name="lists", bufs=1))
        keep = ctx.enter_context(tc.tile_pool(name="keep", bufs=1))
        raw_pool = ctx.enter_context(tc.tile_pool(name="raw", bufs=RAW_BUFS))
        stage = ctx.enter_context(tc.tile_pool(name="stage", bufs=3))
        picks = ctx.enter_context(tc.tile_pool(name="picks", bufs=8))
        weights = ctx.enter_context(tc.tile_pool(name="weights", bufs=2))
        wide_psum = ctx.enter_context(tc.psum_pool(name="wide_psum", bufs=4))
        sum_psum = ctx.enter_context(tc.psum_pool(name="sum_psum", bufs=2))
        slot_psum = ctx.enter_context(tc.psum_pool(name="slot_psum", bufs=1))
        slot_banks = [slot_psum.tile([P, GROUP, C], F32, name="slot_bank%d" % i) for i in range(2)]

        def column_parts(e):
            parts = 2 if e == E - 1 else 1
            return [slice(i * H // parts, (i + 1) * H // parts) for i in range(parts)]

        def load_first(w, e):
            raw = raw_pool.tile([P, PACK, H], F32, name="raw", align_bytes=64)
            rows = w[e].rearrange("(p j) c -> p j c", j=PACK)
            for cols in column_parts(e):
                nc.sync.dma_start(out=raw[:, :, cols], in_=rows[:, :, cols])
            return raw

        w2_rows = w2.rearrange("e (p j) n -> p j e n", j=PACK)

        def load_second(block, e0):
            raw = raw_pool.tile([P, GROUP, PACK, P], F32, name="raw", align_bytes=64)
            for e in range(e0, e0 + GROUP):
                nc.sync.dma_start(out=raw[:, e - e0, :, :], in_=w2_rows[:, :, e, block * P : (block + 1) * P])
            return raw

        def copy_on(engine, dst, src):
            if engine is nc.vector:
                nc.vector.tensor_copy(out=dst, in_=src)
            else:
                nc.scalar.copy(out=dst, in_=src)

        def quantize(values, width, pool, name):
            codes = pool.tile([P, width], U32, name=name + "_codes", align_bytes=64)
            scales = pool.tile([P, width], U8, name=name + "_scales", align_bytes=64)
            nc.vector.quantize_mx(out=codes[:].bitcast(FP8X4), scales=scales[:], in_=values)
            return codes, scales

        def mx(dst, stationary, s_cols, moving, m_cols):
            nc.tensor.matmul_mx(
                out=dst,
                lhsT=stationary[0][:, s_cols].bitcast(FP8X4),
                lhsT_scale=stationary[1][:, s_cols],
                rhs=moving[0][:, m_cols].bitcast(FP8X4),
                rhs_scale=moving[1][:, m_cols],
                start=True,
                stop=True,
            )

        token_scales = keep.tile([P, T], U8, name="token_scales", align_bytes=64)
        nc.gpsimd.memset(token_scales[:].bitcast(I32), 0)
        gate_rows = keep.tile([P, P], F32, name="gate_rows")
        nc.gpsimd.memset(gate_rows[:], 0.0)
        gate_step = BLOCKS * P + 1
        gate_count = TOP * TOKEN_BLOCKS
        nc.scalar.dma_start(
            out=gate_rows[0:gate_count, :],
            in_=gate.rearrange("r n (b p) -> (r n b) p", p=P)[0 : (gate_count - 1) * gate_step + 1 : gate_step, :],
        )
        slot_list = lists.tile([P, SLOTS // 16], U16, name="slot_list")
        nc.sync.dma_start(slot_list[:], offs)
        token_words = keep.tile([P, T], I32, name="token_words", align_bytes=64)
        nc.sync.dma_start(out=token_words[:], in_=x_words[0].rearrange("p t r -> p (t r)").bitcast(I32))
        for q in range(4):
            nc.sync.dma_start(
                out=token_scales[32 * q : 32 * q + 4, :].bitcast(I32),
                in_=x_scales[0, 4 * q : 4 * q + 4, :].bitcast(I32),
            )
        first_raw = {}
        for e in range(2):
            first_raw[0, e] = load_first(w1, e)
            first_raw[1, e] = load_first(w3, e)

        identity = keep.tile([P, P], F32, name="identity")
        make_identity(nc, identity[:])
        gate_turned = sum_psum.tile([P, P], F32, name="back")
        nc.tensor.transpose(gate_turned[:], gate_rows[:], identity[:])
        gate_columns = keep.tile([P, gate_count], F32, name="gate_columns")
        nc.scalar.copy(out=gate_columns[:], in_=gate_turned[:, 0:gate_count])
        gates = keep.tile([P, TOP * T], F32, name="gates")
        for q0 in range(0, gate_count, 4):
            spread = sum_psum.tile([P, 4, P], F32, name="back")
            for q in range(q0, q0 + 4):
                nc.tensor.transpose(
                    spread[:, q - q0, :], gate_columns[:, q : q + 1].to_broadcast([P, P]), identity[:]
                )
            nc.scalar.copy(out=gates[:, q0 * P : (q0 + 4) * P], in_=spread[:].rearrange("p q t -> p (q t)"))

        results = []
        for block in range(BLOCKS):
            result = keep.tile([P, SLOTS + PAD], F32, name="result%d" % block)
            nc.gpsimd.memset(result[:, SLOTS:], 0.0)
            results.append(result)

        slot_tokens = []
        for g in range(SLOTS // GATHER):
            piece = slot_list[:, g * GATHER // 16 : (g + 1) * GATHER // 16]
            words = keep.tile([P, GATHER], U32, name="slot_words%d" % g, align_bytes=64)
            scales = keep.tile([P, GATHER], U8, name="slot_scales%d" % g, align_bytes=64)
            nc.vector.tensor_copy(out=words[:], in_=token_words[:].bitcast(U32).indirect(piece))
            nc.vector.tensor_copy(out=scales[:], in_=token_scales[:].indirect(piece))
            slot_tokens.append((words, scales))

        back_lists = []
        for r, pos in enumerate((pos1, pos2, pos3, pos4)):
            back_list = lists.tile([P, T // 16], U16, name="back_list%d" % r)
            nc.sync.dma_start(back_list[:], pos)
            back_lists.append(back_list)
        scalar_stage = [keep.tile([P, H * PACK], BF16, name="scalar_stage%d" % i, align_bytes=64) for i in range(2)]
        vector_stage = keep.tile([P, H * PACK], BF16, name="vector_stage", align_bytes=64)
        scalar_turns = []

        def next_stage(engine):
            if engine is nc.vector:
                return vector_stage
            scalar_turns.append(0)
            return scalar_stage[len(scalar_turns) % len(scalar_stage)]

        def round_first(raw, engine, e):
            rounded = next_stage(engine)
            for cols in column_parts(e):
                copy_on(
                    engine,
                    rounded[:].rearrange("p (t m j) -> p m j t", t=PACK, j=PACK)[
                        :, cols.start // PACK : cols.stop // PACK, :, :
                    ],
                    raw[:, :, cols].rearrange("p j (m t) -> p m j t", t=PACK),
                )
            return rounded

        def first_product(rounded, e):
            weight = quantize(rounded[:], H, stage, "first")
            sums = wide_psum.tile([P, PACK, C], F32, name="wide")
            tokens = slot_tokens[e * C // GATHER]
            cols = slice(e * C % GATHER, e * C % GATHER + C)
            for t in range(PACK):
                mx(sums[:, t, :], weight, slice(t * P, (t + 1) * P), tokens, cols)
            return sums

        hidden = []
        second_raw = {}

        def rectify(a, relu_a):
            nc.scalar.activation(
                out=relu_a.rearrange("p (s t) -> p s t", t=PACK), in_=a[:].rearrange("p t s -> p s t"), func=ACT.Relu
            )

        def gated_product(relu_a, b, h):
            nc.vector.tensor_tensor(
                out=h.rearrange("p (s t) -> p s t", t=PACK),
                in0=b[:].rearrange("p t s -> p s t"),
                in1=relu_a.rearrange("p (s t) -> p s t", t=PACK),
                op=ALU.mult,
            )

        def first_layer(e, pending):
            rounded_w1 = round_first(first_raw[0, e], nc.scalar, e)
            if pending:
                relu_a = first_raw[0, e][:, 0, :]
                rectify(pending[0], relu_a)
            a = first_product(rounded_w1, e)
            rounded_w3 = round_first(first_raw[1, e], nc.vector, e)
            if pending and e < E - 1:
                h = first_raw[1, e][:, 0, 0 : C * PACK // 2].bitcast(BF16)
                gated_product(relu_a, pending[1], h)
            b = first_product(rounded_w3, e)
            if pending and e == E - 1:
                h = first_raw[1, e][:, 0, 0 : C * PACK // 2].bitcast(BF16)
                gated_product(relu_a, pending[1], h)
            if pending:
                hidden.append(quantize(h, C, keep, "hidden%d" % (e - 1)))
            return a, b

        def finish_first_layer(pending, relu_a):
            rectify(pending[0], relu_a)
            h = first_raw[1, E - 1][:, 1, 0 : C * PACK // 2].bitcast(BF16)
            gated_product(relu_a, pending[1], h)
            hidden.append(quantize(h, C, keep, "hidden%d" % (E - 1)))

        def spent_raw(block, e0):
            return second_raw[block, 0] if e0 >= GROUP else second_raw[block - 1, GROUP]

        def second_step(block, e0, count, sums):
            raw = second_raw[block, e0 - e0 % GROUP]
            engine = nc.vector if (block, e0) in VECTOR_CASTS else nc.scalar
            if block > 0:
                rounded = spent_raw(block, e0)[:, 2:4, :, :].rearrange("p e j n -> p (e j n)").bitcast(BF16)
            else:
                rounded = next_stage(engine)[:, 0 : count * P * PACK]
            at = e0 % GROUP
            copy_on(
                engine,
                rounded.rearrange("p (e c i j) -> p e c j i", e=count, i=4, j=PACK),
                raw[:, at : at + count, :, :].rearrange("p e j (c i) -> p e c j i", i=4),
            )
            weight = quantize(rounded, count * P, stage, "second")
            for d in range(count):
                mx(sums[:, d, :], weight, slice(d * P, (d + 1) * P), hidden[e0 + d], slice(0, C))
            return rounded

        def second_layer(block, e0, count, experts_a_step, copy_engine, bank):
            sums = slot_banks[bank][:, 0:count, :]
            for s in range(0, count, experts_a_step):
                second_step(block, e0 + s, experts_a_step, sums[:, s : s + experts_a_step, :])
            copy_on(
                copy_engine, results[block][:, e0 * C : (e0 + count) * C], sums.rearrange("p e s -> p (e s)")
            )


        def next_block_pair(block, group):
            e0 = group * GROUP
            sums = slot_banks[group]
            spent = second_step(block, e0, GROUP, sums[:])
            nc.scalar.copy(
                out=results[block][:, e0 * C : (e0 + GROUP) * C], in_=sums[:].rearrange("p e s -> p (e s)")
            )
            return spent

        spent_stage = {}

        def weighted_pick(picked, block, r, t0, width):
            offsets = back_lists[r][:, t0 // 16 : (t0 + width) // 16]
            nc.vector.tensor_tensor(
                out=picked,
                in0=results[block][:].indirect(offsets),
                in1=gates[:, r * T + t0 : r * T + t0 + width],
                op=ALU.mult,
            )

        def combine(block, t0, width, casts, gather_after):
            blocks_in_chunk = width // P
            for pair in casts:
                next_block_pair(*pair)
            products = []
            for r in range(TOP):
                if r in gather_after:
                    picked = spent_raw(block + 1, gather_after[r] * GROUP)[:, r, :, :].rearrange("p j n -> p (j n)")[:, 0:width]
                else:
                    picked = picks.tile([P, width], F32, name="picked")[:]
                weighted_pick(picked, block, r, t0, width)
                products.append(picked)
            if casts:
                turned = slot_banks[1][:, 0:blocks_in_chunk, :]
            else:
                turned = wide_psum.tile([P, blocks_in_chunk, P], F32, name="wide")[:]
            for b in range(blocks_in_chunk):
                for r in range(TOP):
                    nc.tensor.matmul(
                        turned[:, b, :],
                        lhsT=products[r][:, b * P : (b + 1) * P],
                        rhs=identity[:],
                        start=(r == 0),
                        stop=(r == TOP - 1),
                        is_transpose=True,
                    )
            room = weights.tile([P, blocks_in_chunk, P], F32, name="weighted")
            nc.scalar.copy(out=room[:], in_=turned)
            total = sum_psum.tile([P, blocks_in_chunk, P], F32, name="back")
            for b in range(blocks_in_chunk):
                nc.tensor.transpose(total[:, b, :], room[:, b, :], identity[:])
            done = stage.tile([P, width], F32, name="done")
            nc.scalar.copy(out=done[:], in_=total[:].rearrange("p b t -> p (b t)"))
            nc.sync.dma_start(out=out[block * P : (block + 1) * P, t0 : t0 + width], in_=done[:])

        def combine_last(block, t0):
            total = None
            for r in range(TOP):
                picked = picks.tile([P, CHUNK], F32, name="picked")
                weighted_pick(picked[:], block, r, t0, CHUNK)
                if r > 0:
                    more = stage.tile([P, CHUNK], F32, name="done")
                    nc.vector.tensor_tensor(out=more[:], in0=total[:], in1=picked[:], op=ALU.add)
                    picked = more
                total = picked
            nc.sync.dma_start(out=out[block * P : (block + 1) * P, t0 : t0 + CHUNK], in_=total[:])

        pending = None
        for e in range(E):
            if e + 2 < E:
                first_raw[0, e + 2] = load_first(w1, e + 2)
                first_raw[1, e + 2] = load_first(w3, e + 2)
            if e == E - 2:
                for block in range(BLOCKS):
                    for e0 in range(0, E, GROUP):
                        second_raw[block, e0] = load_second(block, e0)
            pending = first_layer(e, pending)
        second_layer(0, 0, GROUP, 2, nc.scalar, 0)
        finish_first_layer(pending, second_raw[0, 0][:, 1, :, :].rearrange("p j n -> p (j n)"))
        second_layer(0, GROUP, 2, 1, nc.scalar, 1)
        second_layer(0, E - 2, 2, 1, nc.vector, 0)
        for block in range(BLOCKS - 1):
            pairs = [(block + 1, pair) for pair in range(E // GROUP)]
            combine(block, 0, T // 2, pairs, {2: 0, 3: 0})
            combine(block, T // 2, T // 2, [], {0: 1, 1: 1, 2: 1, 3: 1})
        for t0 in range(0, T - CHUNK, CHUNK):
            combine(BLOCKS - 1, t0, CHUNK, [], {})
        combine_last(BLOCKS - 1, T - CHUNK)
